import numpy as np
import ml_dtypes


def mxq(x, axis, fmt="e4m3"):
    dtype, down = {"e4m3": (ml_dtypes.float8_e4m3fn, 7), "e5m2": (ml_dtypes.float8_e5m2, 14)}[fmt]
    v = np.moveaxis(np.asarray(x, np.float32).astype(ml_dtypes.bfloat16).astype(np.float64), axis, -1)
    blocks = v.reshape(v.shape[:-1] + (-1, 32))
    amax = np.abs(blocks).max(-1, keepdims=True)
    byte = np.maximum(np.where(amax > 0, np.frexp(amax)[1] - 1 + 127, 0) - down, 1)
    scale = np.exp2(byte - 127.0)
    codes = (blocks / scale).astype(np.float32).astype(dtype).astype(np.float64)
    return np.moveaxis((codes * scale).reshape(v.shape), -1, axis)


WIDE = False


def mx_kscale(k):
    if not WIDE:
        return np.ones(k)
    levels = np.array([24, -24, 12, -12, 0])
    if k % 512:
        return np.exp2(np.random.permutation(np.resize(levels, k // 32))).repeat(32)
    a = np.empty((k // 512, 16))
    for p in range(k // 512):
        a[p, :8] = np.random.permutation(np.resize(levels, 8))
        for g in range(8):
            far = levels[np.abs(levels - a[p, g]) >= 10]
            a[p, g + 8] = far[np.random.randint(len(far))]
    return np.exp2(a.ravel()).repeat(32)


def f64(x):
    return np.asarray(x).astype(np.float64)


def striped(idx):
    return np.tile(idx.reshape(-1, 16).T, (8, 1)).astype(np.uint16)


def unstriped(offs):
    return offs[:16].T.reshape(-1).astype(np.int64)


E2M1 = np.array([0.0, 0.5, 1.0, 1.5, 2.0, 3.0, 4.0, 6.0, -0.0, -0.5, -1.0, -1.5, -2.0, -3.0, -4.0, -6.0])


def pack_weight(w, fmt):
    k, n = w.shape
    w = f64(np.asarray(w, np.float32).astype(ml_dtypes.bfloat16)).reshape(k // 32, 32, n)
    amax = np.abs(w).max(1)
    if fmt == "e4m3":
        byte = np.frexp(amax)[1] - 1 + 127 - 7
    else:
        mant, ex = np.frexp(amax / 6.0)
        byte = np.where(mant > 0.5, ex, ex - 1) + 127
    byte = np.clip(np.where(amax > 0, byte, 1), 1, 254)
    scaled = (w * np.exp2(127.0 - byte)[:, None, :]).reshape(k, n).astype(np.float32)
    by_word = np.ascontiguousarray(scaled.reshape(k // 512, 128, 4, n).transpose(0, 1, 3, 2))
    if fmt == "e4m3":
        words = by_word.astype(ml_dtypes.float8_e4m3fn).view(np.uint8)
    else:
        c = by_word.astype(ml_dtypes.float4_e2m1fn).view(np.uint8) & 0xF
        words = (c[..., 0::2] | (c[..., 1::2] << 4)).reshape(k // 512, 128, 2 * n)
    return np.ascontiguousarray(words), np.ascontiguousarray(byte.astype(np.uint8).reshape(k // 512, 16, n))


def unpack_weight(words, scales, fmt):
    g, _, n = scales.shape
    words = np.ascontiguousarray(words).reshape(g, 128, n, -1)
    if fmt == "e4m3":
        vals = words.view(ml_dtypes.float8_e4m3fn).astype(np.float64)
    else:
        nib = np.empty((g, 128, n, 4), np.uint8)
        nib[..., 0::2] = words & 0xF
        nib[..., 1::2] = words >> 4
        vals = E2M1[nib]
    vals = vals * np.repeat(np.exp2(scales.astype(np.float64) - 127.0), 8, axis=1)[..., None]
    return vals.transpose(0, 1, 3, 2).reshape(g * 512, n)


def sigm(f):
    return 1.0 / (1.0 + np.exp(-np.maximum(f, -700.0)))


def gelu(f):
    return 0.5 * f * (1.0 + np.tanh(np.sqrt(2.0 / np.pi) * (f + 0.044715 * f**3)))


K, N, T, J = 1024, 256, 4096, 2048


def setup_inputs():
    n = np.random.standard_normal
    s = mx_kscale(K)[:, None]
    p_tab = pack_weight(n((K, T)) * s, "e4m3")
    p_wh4 = pack_weight(n((K, N)) / np.sqrt(K) / s, "e2m1")
    return {
        "tab_words": p_tab[0],
        "tab_scales": p_tab[1],
        "wg": (n((K, N)) / np.sqrt(K) / s).astype(np.float32),
        "wh4_words": p_wh4[0],
        "wh4_scales": p_wh4[1],
        "whd": (0.4 * (n((K, N)) / np.sqrt(K) / s)).astype(np.float32),
        "bg": (0.3 * n(N) - 1.0).astype(np.float32),
        "rT": (n((N, T))).astype(np.float32),
        "offs": striped(np.random.permutation(T)[:J]),
    }


def reference(tab_words, tab_scales, wg, wh4_words, wh4_scales, whd, bg, rT, offs):
    idx = unstriped(offs)
    tab_ = unpack_weight(tab_words, tab_scales, "e4m3")[:, idx]
    wg_ = mxq(f64(wg), 0, "e4m3")
    wh4_ = unpack_weight(wh4_words, wh4_scales, "e2m1")
    whd_ = mxq(f64(whd), 0, "e4m3")
    ga = wg_.T @ tab_
    gate = sigm(ga + f64(bg)[:, None])
    ha = wh4_.T @ tab_ + whd_.T @ tab_
    return f64(rT)[:, idx] + gate * (gelu(ha) - f64(rT)[:, idx])

@@ -1,0 +1,214 @@
+from contextlib import ExitStack
+
+import concourse.mybir as mybir
+
+K, N, T, J = 1024, 256, 4096, 2048
+FLOPS = 3 * 2 * K * N * J
+
+F32 = mybir.dt.float32
+BF16 = mybir.dt.bfloat16
+I32 = mybir.dt.int32
+U32 = mybir.dt.uint32
+U16 = mybir.dt.uint16
+U8 = mybir.dt.uint8
+FP8X4 = mybir.dt.float8_e4m3fn_x4
+FP4X4 = mybir.dt.float4_e2m1fn_x4
+ACT = mybir.ActivationFunctionType
+ALU = mybir.AluOpType
+
+P = 128
+PACK = 4
+PASSES = K // (P * PACK)
+HALVES = N // P
+BANK = 512
+CHUNKS = J // BANK
+LIST_ROWS = 16
+SCALE_ROWS = 16
+SCALE_BASE = P - PASSES * SCALE_ROWS
+PIECES = [(0, 0, 512), (0, 512, 512), (0, 1024, 1024), (1, 0, 1024), (1, 1024, 512), (1, 1536, 256), (1, 1792, 256)]
+
+
+def tile_list_hwayt_dl_gelu_kernel(
+    tc, tab_words, tab_scales, wg, wh4_words, wh4_scales, whd, bg, rT, offs, out
+):
+    nc = tc.nc
+    with ExitStack() as ctx:
+        keep = ctx.enter_context(tc.tile_pool(name="keep", bufs=1))
+        psum = ctx.enter_context(tc.psum_pool(name="psum", bufs=4))
+
+        offsets = keep.tile([P, J // LIST_ROWS], U16, name="offsets")
+
+        def listed(window, j0, count):
+            return window.indirect(offsets[:, j0 // LIST_ROWS : (j0 + count) // LIST_ROWS])
+
+        nc.sync.dma_start(offsets[:], offs)
+        scale_window = keep.tile([P, T // 4], I32, name="scale_window", tag="window1", align_bytes=64)
+        nc.sync.dma_start(scale_window[SCALE_BASE:P, :], tab_scales.rearrange("a q t -> (a q) t").bitcast(I32))
+        nc.vector.memset(scale_window[0:SCALE_BASE, :], 0)
+
+        warm = keep.tile([P, 8], F32, name="warm")
+        nc.gpsimd.memset(warm[:], 0.0)
+        nc.scalar.activation(warm[:, 4:5], warm[:, 0:1], ACT.Gelu_apprx_tanh)
+
+        def load_words(a):
+            window = keep.tile([P, T], I32, name=f"word_window{a}", tag=f"window{a}", align_bytes=64)
+            nc.sync.dma_start(window[:], tab_words[a].rearrange("p t i -> p (t i)").bitcast(I32))
+            return window
+
+        def load_weight(w, a, name):
+            raw = keep.tile([P, PACK, N], F32, name=f"{name}_raw{a}", tag=f"{name}_raw")
+            nc.sync.dma_start(raw[:], w[a * P * PACK : (a + 1) * P * PACK, :].rearrange("(p i) n -> p i n", i=PACK))
+            return raw
+
+        def round_weight(raw, a, name):
+            grouped = keep.tile([P, N, PACK], BF16, name=f"{name}_bf16_{a}", align_bytes=64)
+            nc.scalar.copy(
+                grouped[:].rearrange("p (c e) i -> p c i e", e=4),
+                raw[:].rearrange("p i (c e) -> p c i e", e=4),
+            )
+            return grouped
+
+        def quantise_weight(grouped, a, name):
+            codes = keep.tile([P, N], U32, name=f"{name}_codes{a}", align_bytes=64)
+            scales = keep.tile([P, N], U8, name=f"{name}_scales{a}", align_bytes=64)
+            nc.vector.quantize_mx(
+                out=codes[:].bitcast(FP8X4), scales=scales[:], in_=grouped[:].rearrange("p n i -> p (n i)")
+            )
+            return codes, scales
+
+        word_window0 = load_words(0)
+        wg_raw0 = load_weight(wg, 0, "wg")
+        whd_raw0 = load_weight(whd, 0, "whd")
+
+        wh4_codes = keep.tile([P, PASSES, 2 * N], U8, name="wh4_codes", align_bytes=64)
+        wh4_planes = keep.tile([P, PASSES, N], U8, name="wh4_planes", align_bytes=64)
+        bias = keep.tile([P, HALVES], F32, name="bias")
+        half_bias = keep.tile([P, HALVES], F32, name="half_bias")
+        nc.gpsimd.memset(wh4_planes[:].bitcast(I32), 0)
+        nc.gpsimd.dma_start(wh4_codes[:].bitcast(I32), wh4_words.rearrange("a p n -> p a n").bitcast(I32))
+        wh4_rows = wh4_scales.bitcast(I32).rearrange("a (q r) n -> r q a n", r=4)
+        for r in range(4):
+            nc.gpsimd.dma_start(wh4_planes[r:P:32, :, :].bitcast(I32), wh4_rows[r])
+        with nc.allow_non_contiguous_dma(reason="one bias value a partition"):
+            nc.gpsimd.dma_start(bias[:], bg.rearrange("(h p) -> p h", p=P))
+        nc.scalar.mul(half_bias[:], bias[:], 0.5)
+
+        tab_planes = keep.tile([P, PASSES, J], U8, name="tab_planes", align_bytes=64)
+        nc.vector.memset(tab_planes[:].bitcast(I32), 0)
+
+        picked_scales = keep.tile([P, J], U8, name="picked_scales", align_bytes=64)
+        nc.vector.tensor_copy(picked_scales[:], listed(scale_window[:].bitcast(U8), 0, J))
+
+        def move_plane(a):
+            first = SCALE_BASE + a * SCALE_ROWS
+            for r in range(4):
+                nc.sync.dma_start(
+                    tab_planes[r:P:32, a, :].bitcast(I32),
+                    picked_scales[first + r : first + SCALE_ROWS : 4, :].bitcast(I32),
+                )
+
+        move_plane(0)
+        word_window1 = load_words(1)
+        move_plane(1)
+
+        picked_words = [keep.tile([P, J], U32, name=f"picked_words{a}", align_bytes=64) for a in range(PASSES)]
+
+        def gather_words(window, a, j0, count):
+            nc.vector.tensor_copy(picked_words[a][:, j0 : j0 + count], listed(window[:].bitcast(U32), j0, count))
+
+        wg_bf16_0 = round_weight(wg_raw0, 0, "wg")
+        whd_bf16_0 = round_weight(whd_raw0, 0, "whd")
+        gather_words(word_window0, 0, 0, J // 2)
+        wg_mx = [quantise_weight(wg_bf16_0, 0, "wg")]
+        gather_words(word_window0, 0, J // 2, J // 2)
+        whd_mx = [quantise_weight(whd_bf16_0, 0, "whd")]
+
+        wg_raw1 = load_weight(wg, 1, "wg")
+        whd_raw1 = load_weight(whd, 1, "whd")
+        carried = []
+        carried.append(keep.tile([P, T], F32, name="carried0", tag="window0", align_bytes=64))
+        nc.sync.dma_start(carried[0][:], rT[0:P, :])
+
+        def table_pass(acc, codes, scales, a, c, start, stop):
+            cols = slice(c * BANK, (c + 1) * BANK)
+            nc.tensor.matmul_mx(
+                out=acc[:],
+                lhsT=codes,
+                lhsT_scale=scales,
+                rhs=picked_words[a][:, cols].bitcast(FP8X4),
+                rhs_scale=tab_planes[:, a, cols],
+                start=start,
+                stop=stop,
+            )
+
+        def products(ga, ha, a, h, c):
+            rows = slice(h * P, (h + 1) * P)
+            first, last = a == 0, a == PASSES - 1
+            table_pass(ga, wg_mx[a][0][:, rows].bitcast(FP8X4), wg_mx[a][1][:, rows], a, c, first, last)
+            fp4_codes = wh4_codes[:, a, 2 * h * P : 2 * (h + 1) * P].bitcast(FP4X4)
+            table_pass(ha, fp4_codes, wh4_planes[:, a, rows], a, c, first, False)
+            table_pass(ha, whd_mx[a][0][:, rows].bitcast(FP8X4), whd_mx[a][1][:, rows], a, c, False, last)
+
+        def open_banks():
+            ga = psum.tile([P, BANK], F32, name="ga")
+            ha = psum.tile([P, BANK], F32, name="ha")
+            return ga, ha
+
+        tanh_half = [keep.tile([P, J], F32, name=f"tanh_half{h}") for h in range(HALVES)]
+        keep_share = [keep.tile([P, J], F32, name=f"keep_share{h}") for h in range(HALVES)]
+        made = [keep.tile([P, J], F32, name=f"made{h}") for h in range(HALVES)]
+
+        def activations(ga, ha, h, c):
+            cols = slice(c * BANK, (c + 1) * BANK)
+            nc.scalar.activation(tanh_half[h][:, cols], ga[:], ACT.Tanh, bias=half_bias[:, h : h + 1], scale=0.5)
+            nc.scalar.activation(made[h][:, cols], ha[:], ACT.Gelu_apprx_tanh)
+            nc.scalar.activation(keep_share[h][:, cols], tanh_half[h][:, cols], ACT.Copy, bias=0.5, scale=-0.5)
+
+        banks = [open_banks() for c in range(CHUNKS)]
+        for c in range(CHUNKS):
+            products(banks[c][0], banks[c][1], 0, 0, c)
+
+        wg_bf16_1 = round_weight(wg_raw1, 1, "wg")
+        whd_bf16_1 = round_weight(whd_raw1, 1, "whd")
+        gather_words(word_window1, 1, 0, BANK)
+        gather_words(word_window1, 1, BANK, BANK)
+        wg_mx.append(quantise_weight(wg_bf16_1, 1, "wg"))
+        gather_words(word_window1, 1, 2 * BANK, BANK)
+        whd_mx.append(quantise_weight(whd_bf16_1, 1, "whd"))
+        gather_words(word_window1, 1, 3 * BANK, BANK)
+
+        carried.append(keep.tile([P, T], F32, name="carried1", tag="window1", align_bytes=64))
+        nc.sync.dma_start(carried[1][:], rT[P : 2 * P, :])
+
+        for c in range(CHUNKS):
+            products(banks[c][0], banks[c][1], 1, 0, c)
+            activations(banks[c][0], banks[c][1], 0, c)
+        for c in range(CHUNKS):
+            ga, ha = open_banks()
+            for a in range(PASSES):
+                products(ga, ha, a, 1, c)
+            activations(ga, ha, 1, c)
+
+        def shares(u):
+            h, j0, count = PIECES[u]
+            cols = slice(j0, j0 + count)
+            new_part = keep.tile([P, count], F32, name=f"new_part{u}")
+            old_part = keep.tile([P, count], F32, name=f"old_part{u}")
+            nc.vector.scalar_tensor_tensor(
+                new_part[:], tanh_half[h][:, cols], 1.0, made[h][:, cols], ALU.add, ALU.mult
+            )
+            nc.vector.tensor_tensor(old_part[:], listed(carried[h][:], j0, count), keep_share[h][:, cols], ALU.mult)
+            return new_part, old_part
+
+        def finish(u, new_part, old_part):
+            h, j0, count = PIECES[u]
+            result = keep.tile([P, count], F32, name=f"result{u}")
+            nc.vector.scalar_tensor_tensor(result[:], new_part[:], 0.5, old_part[:], ALU.mult, ALU.add)
+            nc.sync.dma_start(out[h * P : (h + 1) * P, j0 : j0 + count], result[:])
+
+        pending = shares(0)
+        for u in range(1, len(PIECES)):
+            following = shares(u)
+            finish(u - 1, *pending)
+            pending = following
+        finish(len(PIECES) - 1, *pending)

@@ -25,7 +25,7 @@ CHUNKS = J // BANK
 LIST_ROWS = 16
 SCALE_ROWS = 16
 SCALE_BASE = P - PASSES * SCALE_ROWS
-PIECES = [(0, 0, 512), (0, 512, 512), (0, 1024, 1024), (1, 0, 1024), (1, 1024, 512), (1, 1536, 256), (1, 1792, 256)]
+PIECES = [(0, 0, 512), (0, 512, 512), (0, 1024, 512), (0, 1536, 512), (1, 0, 512), (1, 512, 512), (1, 1024, 512), (1, 1536, 256), (1, 1792, 256)]
 
 
 def tile_list_hwayt_dl_gelu_kernel(
@@ -44,6 +44,8 @@ def tile_list_hwayt_dl_gelu_kernel(
         nc.sync.dma_start(offsets[:], offs)
         scale_window = keep.tile([P, T // 4], I32, name="scale_window", tag="window1", align_bytes=64)
         nc.sync.dma_start(scale_window[SCALE_BASE:P, :], tab_scales.rearrange("a q t -> (a q) t").bitcast(I32))
+        wh4_planes = keep.tile([P, PASSES, N], U8, name="wh4_planes", align_bytes=64)
+        nc.vector.memset(wh4_planes[:].bitcast(I32), 0)
         nc.vector.memset(scale_window[0:SCALE_BASE, :], 0)
 
         warm = keep.tile([P, 8], F32, name="warm")
@@ -55,46 +57,47 @@ def tile_list_hwayt_dl_gelu_kernel(
             nc.sync.dma_start(window[:], tab_words[a].rearrange("p t i -> p (t i)").bitcast(I32))
             return window
 
-        def load_weight(w, a, name):
-            raw = keep.tile([P, PACK, N], F32, name=f"{name}_raw{a}", tag=f"{name}_raw")
-            nc.sync.dma_start(raw[:], w[a * P * PACK : (a + 1) * P * PACK, :].rearrange("(p i) n -> p i n", i=PACK))
+        def load_whd(a):
+            raw = keep.tile([P, PACK, N], F32, name=f"whd_raw{a}", tag="whd_raw")
+            nc.sync.dma_start(raw[:], whd[a * P * PACK : (a + 1) * P * PACK, :].rearrange("(p i) n -> p i n", i=PACK))
             return raw
 
-        def round_weight(raw, a, name):
-            grouped = keep.tile([P, N, PACK], BF16, name=f"{name}_bf16_{a}", align_bytes=64)
-            nc.scalar.copy(
-                grouped[:].rearrange("p (c e) i -> p c i e", e=4),
-                raw[:].rearrange("p i (c e) -> p c i e", e=4),
-            )
-            return grouped
+        def mx_tiles(name):
+            grouped = keep.tile([P, N, PACK], BF16, name=f"{name}_bf16", tag=f"{name}_bf16", align_bytes=64)
+            codes = keep.tile([P, N], U32, name=f"{name}_codes", align_bytes=64)
+            scales = keep.tile([P, N], U8, name=f"{name}_scales", align_bytes=64)
+            return grouped, codes, scales
 
-        def quantise_weight(grouped, a, name):
-            codes = keep.tile([P, N], U32, name=f"{name}_codes{a}", align_bytes=64)
-            scales = keep.tile([P, N], U8, name=f"{name}_scales{a}", align_bytes=64)
-            nc.vector.quantize_mx(
-                out=codes[:].bitcast(FP8X4), scales=scales[:], in_=grouped[:].rearrange("p n i -> p (n i)")
+        def round_weight(raw, mx):
+            nc.scalar.copy(
+                mx[0][:].rearrange("p (c e) i -> p c i e", e=4),
+                raw.rearrange("p i (c e) -> p c i e", e=4),
             )
-            return codes, scales
+
+        def quantise_weight(mx):
+            nc.vector.quantize_mx(
+                out=mx[1][:].bitcast(FP8X4), scales=mx[2][:], in_=mx[0][:].rearrange("p n i -> p (n i)")
+            )
 
         word_window0 = load_words(0)
-        wg_raw0 = load_weight(wg, 0, "wg")
-        whd_raw0 = load_weight(whd, 0, "whd")
 
         wh4_codes = keep.tile([P, PASSES, 2 * N], U8, name="wh4_codes", align_bytes=64)
-        wh4_planes = keep.tile([P, PASSES, N], U8, name="wh4_planes", align_bytes=64)
         bias = keep.tile([P, HALVES], F32, name="bias")
         half_bias = keep.tile([P, HALVES], F32, name="half_bias")
-        nc.gpsimd.memset(wh4_planes[:].bitcast(I32), 0)
-        nc.gpsimd.dma_start(wh4_codes[:].bitcast(I32), wh4_words.rearrange("a p n -> p a n").bitcast(I32))
+        nc.sync.dma_start(wh4_codes[:].bitcast(I32), wh4_words.rearrange("a p n -> p a n").bitcast(I32))
         wh4_rows = wh4_scales.bitcast(I32).rearrange("a (q r) n -> r q a n", r=4)
         for r in range(4):
-            nc.gpsimd.dma_start(wh4_planes[r:P:32, :, :].bitcast(I32), wh4_rows[r])
+            nc.sync.dma_start(wh4_planes[r:P:32, :, :].bitcast(I32), wh4_rows[r])
+        whd_raw0 = load_whd(0)
+        wg_raw = keep.tile([P, PASSES, PACK, N], F32, name="wg_raw")
+        nc.sync.dma_start(wg_raw[:], wg.rearrange("(a p i) n -> p a i n", p=P, i=PACK))
         with nc.allow_non_contiguous_dma(reason="one bias value a partition"):
             nc.gpsimd.dma_start(bias[:], bg.rearrange("(h p) -> p h", p=P))
-        nc.scalar.mul(half_bias[:], bias[:], 0.5)
+        nc.gpsimd.tensor_scalar(half_bias[:], bias[:], 0.5, 0.0, ALU.mult, ALU.add)
 
-        tab_planes = keep.tile([P, PASSES, J], U8, name="tab_planes", align_bytes=64)
-        nc.vector.memset(tab_planes[:].bitcast(I32), 0)
+        tab_planes = [keep.tile([P, J], U8, name=f"tab_plane{a}", align_bytes=64) for a in range(PASSES)]
+        for a in range(PASSES):
+            nc.vector.memset(tab_planes[a][:].bitcast(I32), 0)
 
         picked_scales = keep.tile([P, J], U8, name="picked_scales", align_bytes=64)
         nc.vector.tensor_copy(picked_scales[:], listed(scale_window[:].bitcast(U8), 0, J))
@@ -103,7 +106,7 @@ def tile_list_hwayt_dl_gelu_kernel(
             first = SCALE_BASE + a * SCALE_ROWS
             for r in range(4):
                 nc.sync.dma_start(
-                    tab_planes[r:P:32, a, :].bitcast(I32),
+                    tab_planes[a][r:P:32, :].bitcast(I32),
                     picked_scales[first + r : first + SCALE_ROWS : 4, :].bitcast(I32),
                 )
 
@@ -111,22 +114,33 @@ def tile_list_hwayt_dl_gelu_kernel(
         word_window1 = load_words(1)
         move_plane(1)
 
-        picked_words = [keep.tile([P, J], U32, name=f"picked_words{a}", align_bytes=64) for a in range(PASSES)]
+        picked_words = {}
 
-        def gather_words(window, a, j0, count):
-            nc.vector.tensor_copy(picked_words[a][:, j0 : j0 + count], listed(window[:].bitcast(U32), j0, count))
+        def gather_first_words():
+            picked = keep.tile([P, J], U32, name="picked_words0", align_bytes=64)
+            nc.vector.tensor_copy(picked[:], listed(word_window0[:].bitcast(U32), 0, J))
+            for c in range(CHUNKS):
+                picked_words[0, c] = picked[:, c * BANK : (c + 1) * BANK]
 
-        wg_bf16_0 = round_weight(wg_raw0, 0, "wg")
-        whd_bf16_0 = round_weight(whd_raw0, 0, "whd")
-        gather_words(word_window0, 0, 0, J // 2)
-        wg_mx = [quantise_weight(wg_bf16_0, 0, "wg")]
-        gather_words(word_window0, 0, J // 2, J // 2)
-        whd_mx = [quantise_weight(whd_bf16_0, 0, "whd")]
+        def gather_second_words(c, tag):
+            picked = keep.tile([P, BANK], U32, name=f"picked_words1_{c}", tag=tag, align_bytes=64)
+            nc.vector.tensor_copy(picked[:], listed(word_window1[:].bitcast(U32), c * BANK, BANK))
+            picked_words[1, c] = picked[:]
 
-        wg_raw1 = load_weight(wg, 1, "wg")
-        whd_raw1 = load_weight(whd, 1, "whd")
-        carried = []
-        carried.append(keep.tile([P, T], F32, name="carried0", tag="window0", align_bytes=64))
+        wg_mx = [mx_tiles(f"wg{a}") for a in range(PASSES)]
+        whd_mx = [mx_tiles(f"whd{a}") for a in range(PASSES)]
+        half_cols = [slice(h * P, (h + 1) * P) for h in range(HALVES)]
+
+        round_weight(whd_raw0[:], whd_mx[0])
+        for a in range(PASSES):
+            round_weight(wg_raw[:, a], wg_mx[a])
+        gather_first_words()
+        quantise_weight(whd_mx[0])
+        for a in range(PASSES):
+            quantise_weight(wg_mx[a])
+
+        whd_raw1 = load_whd(1)
+        carried = [keep.tile([P, T], F32, name="carried0", tag="window0", align_bytes=64)]
         nc.sync.dma_start(carried[0][:], rT[0:P, :])
 
         def table_pass(acc, codes, scales, a, c, start, stop):
@@ -135,80 +149,129 @@ def tile_list_hwayt_dl_gelu_kernel(
                 out=acc[:],
                 lhsT=codes,
                 lhsT_scale=scales,
-                rhs=picked_words[a][:, cols].bitcast(FP8X4),
-                rhs_scale=tab_planes[:, a, cols],
+                rhs=picked_words[a, c].bitcast(FP8X4),
+                rhs_scale=tab_planes[a][:, cols],
                 start=start,
                 stop=stop,
             )
 
-        def products(ga, ha, a, h, c):
-            rows = slice(h * P, (h + 1) * P)
-            first, last = a == 0, a == PASSES - 1
-            table_pass(ga, wg_mx[a][0][:, rows].bitcast(FP8X4), wg_mx[a][1][:, rows], a, c, first, last)
-            fp4_codes = wh4_codes[:, a, 2 * h * P : 2 * (h + 1) * P].bitcast(FP4X4)
-            table_pass(ha, fp4_codes, wh4_planes[:, a, rows], a, c, first, False)
-            table_pass(ha, whd_mx[a][0][:, rows].bitcast(FP8X4), whd_mx[a][1][:, rows], a, c, False, last)
+        banks = {}
 
-        def open_banks():
-            ga = psum.tile([P, BANK], F32, name="ga")
-            ha = psum.tile([P, BANK], F32, name="ha")
-            return ga, ha
+        def open_banks(h, c):
+            banks[h, c] = (psum.tile([P, BANK], F32, name="ga"), psum.tile([P, BANK], F32, name="ha"))
 
-        tanh_half = [keep.tile([P, J], F32, name=f"tanh_half{h}") for h in range(HALVES)]
-        keep_share = [keep.tile([P, J], F32, name=f"keep_share{h}") for h in range(HALVES)]
-        made = [keep.tile([P, J], F32, name=f"made{h}") for h in range(HALVES)]
+        def wg_pass(a, h, c):
+            rows = half_cols[h]
+            table_pass(banks[h, c][0], wg_mx[a][1][:, rows].bitcast(FP8X4), wg_mx[a][2][:, rows], a, c, a == 0, a == 1)
 
-        def activations(ga, ha, h, c):
-            cols = slice(c * BANK, (c + 1) * BANK)
-            nc.scalar.activation(tanh_half[h][:, cols], ga[:], ACT.Tanh, bias=half_bias[:, h : h + 1], scale=0.5)
-            nc.scalar.activation(made[h][:, cols], ha[:], ACT.Gelu_apprx_tanh)
-            nc.scalar.activation(keep_share[h][:, cols], tanh_half[h][:, cols], ACT.Copy, bias=0.5, scale=-0.5)
+        def wh4_pass(a, h, c):
+            codes = wh4_codes[:, a, 2 * h * P : 2 * (h + 1) * P].bitcast(FP4X4)
+            table_pass(banks[h, c][1], codes, wh4_planes[:, a, half_cols[h]], a, c, a == 0, False)
 
-        banks = [open_banks() for c in range(CHUNKS)]
+        def whd_pass(a, h, c):
+            rows = half_cols[h]
+            table_pass(banks[h, c][1], whd_mx[a][1][:, rows].bitcast(FP8X4), whd_mx[a][2][:, rows], a, c, False, a == 1)
+
+        tanh_half = {}
+        keep_share = {}
+        made = {}
+
+        def gate_tanh(h, c, tag):
+            tanh_half[h, c] = keep.tile([P, BANK], F32, name=f"tanh_half{h}_{c}", tag=tag)
+            nc.scalar.activation(
+                tanh_half[h, c][:], banks[h, c][0][:], ACT.Tanh, bias=half_bias[:, h : h + 1], scale=0.5
+            )
+
+        def gelu(h, c):
+            made[h, c] = keep.tile([P, BANK], F32, name=f"made{h}_{c}")
+            nc.scalar.activation(made[h, c][:], banks[h, c][1][:], ACT.Gelu_apprx_tanh)
+
+        def gate_rest(h, c):
+            keep_share[h, c] = keep.tile([P, BANK], F32, name=f"keep_share{h}_{c}", tag=f"keep_share{h}_{c}")
+            nc.scalar.activation(keep_share[h, c][:], tanh_half[h, c][:], ACT.Copy, bias=0.5, scale=-0.5)
+
         for c in range(CHUNKS):
-            products(banks[c][0], banks[c][1], 0, 0, c)
+            open_banks(0, c)
+            wh4_pass(0, 0, c)
+            whd_pass(0, 0, c)
+            wg_pass(0, 0, c)
 
-        wg_bf16_1 = round_weight(wg_raw1, 1, "wg")
-        whd_bf16_1 = round_weight(whd_raw1, 1, "whd")
-        gather_words(word_window1, 1, 0, BANK)
-        gather_words(word_window1, 1, BANK, BANK)
-        wg_mx.append(quantise_weight(wg_bf16_1, 1, "wg"))
-        gather_words(word_window1, 1, 2 * BANK, BANK)
-        whd_mx.append(quantise_weight(whd_bf16_1, 1, "whd"))
-        gather_words(word_window1, 1, 3 * BANK, BANK)
+        round_weight(whd_raw1[:], whd_mx[1])
+        for c in range(3):
+            gather_second_words(c, f"picked_words1_{c}")
+        quantise_weight(whd_mx[1])
+        gather_second_words(3, "whd1_bf16")
+        for c in range(2):
+            wg_pass(1, 0, c)
+            wh4_pass(1, 0, c)
+            gate_tanh(0, c, "whd_raw" if c == 0 else f"tanh_half0_{c}")
+        for c in range(2):
+            whd_pass(1, 0, c)
+            gelu(0, c)
+        for c in range(2):
+            gate_rest(0, c)
 
         carried.append(keep.tile([P, T], F32, name="carried1", tag="window1", align_bytes=64))
         nc.sync.dma_start(carried[1][:], rT[P : 2 * P, :])
 
+        for c in range(2, CHUNKS):
+            wg_pass(1, 0, c)
+            wh4_pass(1, 0, c)
+            whd_pass(1, 0, c)
+            gate_tanh(0, c, f"tanh_half0_{c}")
+            gelu(0, c)
+            gate_rest(0, c)
         for c in range(CHUNKS):
-            products(banks[c][0], banks[c][1], 1, 0, c)
-            activations(banks[c][0], banks[c][1], 0, c)
-        for c in range(CHUNKS):
-            ga, ha = open_banks()
+            open_banks(1, c)
             for a in range(PASSES):
-                products(ga, ha, a, 1, c)
-            activations(ga, ha, 1, c)
+                wg_pass(a, 1, c)
+            for a in range(PASSES):
+                wh4_pass(a, 1, c)
+                whd_pass(a, 1, c)
+            gate_tanh(1, c, f"tanh_half1_{c}")
+            gelu(1, c)
+            gate_rest(1, c)
 
-        def shares(u):
+        new_part = {}
+        old_part = {}
+
+        def bank_of(u):
             h, j0, count = PIECES[u]
-            cols = slice(j0, j0 + count)
-            new_part = keep.tile([P, count], F32, name=f"new_part{u}")
-            old_part = keep.tile([P, count], F32, name=f"old_part{u}")
+            return (h, j0 // BANK), slice(j0 % BANK, j0 % BANK + count)
+
+        def new_share(u):
+            bank, cols = bank_of(u)
+            tag = "keep_share%d_%d" % bank_of(u - 2)[0] if 2 <= u < len(PIECES) - 1 else f"new_part{u}"
+            new_part[u] = keep.tile([P, PIECES[u][2]], F32, name=f"new_part{u}", tag=tag)
             nc.vector.scalar_tensor_tensor(
-                new_part[:], tanh_half[h][:, cols], 1.0, made[h][:, cols], ALU.add, ALU.mult
+                new_part[u][:], tanh_half[bank][:, cols], 1.0, made[bank][:, cols], ALU.add, ALU.mult
             )
-            nc.vector.tensor_tensor(old_part[:], listed(carried[h][:], j0, count), keep_share[h][:, cols], ALU.mult)
-            return new_part, old_part
 
-        def finish(u, new_part, old_part):
+        def old_share(u):
             h, j0, count = PIECES[u]
-            result = keep.tile([P, count], F32, name=f"result{u}")
-            nc.vector.scalar_tensor_tensor(result[:], new_part[:], 0.5, old_part[:], ALU.mult, ALU.add)
+            bank, cols = bank_of(u)
+            old_part[u] = keep.tile([P, count], F32, name=f"old_part{u}")
+            nc.vector.tensor_tensor(
+                old_part[u][:], listed(carried[h][:], j0, count), keep_share[bank][:, cols], ALU.mult
+            )
+
+        def finish(u, tag):
+            h, j0, count = PIECES[u]
+            result = keep.tile([P, count], F32, name=f"result{u}", tag=tag)
+            nc.vector.scalar_tensor_tensor(result[:], new_part[u][:], 0.5, old_part[u][:], ALU.mult, ALU.add)
             nc.sync.dma_start(out[h * P : (h + 1) * P, j0 : j0 + count], result[:])
 
-        pending = shares(0)
-        for u in range(1, len(PIECES)):
-            following = shares(u)
-            finish(u - 1, *pending)
-            pending = following
-        finish(len(PIECES) - 1, *pending)
+        last = len(PIECES) - 1
+        new_share(0)
+        new_share(1)
+        old_share(0)
+        for u in range(1, last - 1):
+            old_share(u)
+            finish(u - 1, "tanh_half%d_%d" % bank_of(u)[0])
+            new_share(u + 1)
+        new_share(last)
+        old_share(last - 1)
+        finish(last - 2, "tanh_half%d_%d" % bank_of(last)[0])
+        old_share(last)
+        finish(last - 1, "result_last0")
+        finish(last, "result_last1")

@@ -1,6 +1,7 @@
 from contextlib import ExitStack
 
 import concourse.mybir as mybir
+from concourse.masks import make_identity
 
 K, N, T, J = 1024, 256, 4096, 2048
 FLOPS = 3 * 2 * K * N * J
@@ -25,6 +26,7 @@ CHUNKS = J // BANK
 LIST_ROWS = 16
 SCALE_ROWS = 16
 SCALE_BASE = P - PASSES * SCALE_ROWS
+SUMMED_IN_PSUM = (2, 3, 4)
 PIECES = [(0, 0, 512), (0, 512, 512), (0, 1024, 512), (0, 1536, 512), (1, 0, 512), (1, 512, 512), (1, 1024, 512), (1, 1536, 256), (1, 1792, 256)]
 
 
@@ -34,7 +36,7 @@ def tile_list_hwayt_dl_gelu_kernel(
     nc = tc.nc
     with ExitStack() as ctx:
         keep = ctx.enter_context(tc.tile_pool(name="keep", bufs=1))
-        psum = ctx.enter_context(tc.psum_pool(name="psum", bufs=4))
+        psum = ctx.enter_context(tc.psum_pool(name="psum", bufs=1))
 
         offsets = keep.tile([P, J // LIST_ROWS], U16, name="offsets")
 
@@ -52,15 +54,13 @@ def tile_list_hwayt_dl_gelu_kernel(
         nc.gpsimd.memset(warm[:], 0.0)
         nc.scalar.activation(warm[:, 4:5], warm[:, 0:1], ACT.Gelu_apprx_tanh)
 
+        identity = keep.tile([P, P], F32, name="identity")
+        make_identity(nc, identity[:])
+
         def load_words(a):
             window = keep.tile([P, T], I32, name=f"word_window{a}", tag=f"window{a}", align_bytes=64)
             nc.sync.dma_start(window[:], tab_words[a].rearrange("p t i -> p (t i)").bitcast(I32))
             return window
-
-        def load_whd(a):
-            raw = keep.tile([P, PACK, N], F32, name=f"whd_raw{a}", tag="whd_raw")
-            nc.sync.dma_start(raw[:], whd[a * P * PACK : (a + 1) * P * PACK, :].rearrange("(p i) n -> p i n", i=PACK))
-            return raw
 
         def mx_tiles(name):
             grouped = keep.tile([P, N, PACK], BF16, name=f"{name}_bf16", tag=f"{name}_bf16", align_bytes=64)
@@ -88,8 +88,7 @@ def tile_list_hwayt_dl_gelu_kernel(
         wh4_rows = wh4_scales.bitcast(I32).rearrange("a (q r) n -> r q a n", r=4)
         for r in range(4):
             nc.sync.dma_start(wh4_planes[r:P:32, :, :].bitcast(I32), wh4_rows[r])
-        whd_raw0 = load_whd(0)
-        wg_raw = keep.tile([P, PASSES, PACK, N], F32, name="wg_raw")
+        wg_raw = keep.tile([P, PASSES, PACK, N], F32, name="wg_raw", tag="wg_raw")
         nc.sync.dma_start(wg_raw[:], wg.rearrange("(a p i) n -> p a i n", p=P, i=PACK))
         with nc.allow_non_contiguous_dma(reason="one bias value a partition"):
             nc.gpsimd.dma_start(bias[:], bg.rearrange("(h p) -> p h", p=P))
@@ -131,15 +130,17 @@ def tile_list_hwayt_dl_gelu_kernel(
         whd_mx = [mx_tiles(f"whd{a}") for a in range(PASSES)]
         half_cols = [slice(h * P, (h + 1) * P) for h in range(HALVES)]
 
-        round_weight(whd_raw0[:], whd_mx[0])
         for a in range(PASSES):
             round_weight(wg_raw[:, a], wg_mx[a])
         gather_first_words()
-        quantise_weight(whd_mx[0])
         for a in range(PASSES):
             quantise_weight(wg_mx[a])
 
-        whd_raw1 = load_whd(1)
+        whd_raw = keep.tile([P, PASSES, PACK, N], F32, name="whd_raw", tag="wg_raw")
+        for a in range(PASSES):
+            nc.sync.dma_start(
+                whd_raw[:, a], whd[a * P * PACK : (a + 1) * P * PACK, :].rearrange("(p i) n -> p i n", i=PACK)
+            )
         carried = [keep.tile([P, T], F32, name="carried0", tag="window0", align_bytes=64)]
         nc.sync.dma_start(carried[0][:], rT[0:P, :])
 
@@ -158,7 +159,10 @@ def tile_list_hwayt_dl_gelu_kernel(
         banks = {}
 
         def open_banks(h, c):
-            banks[h, c] = (psum.tile([P, BANK], F32, name="ga"), psum.tile([P, BANK], F32, name="ha"))
+            banks[h, c] = (
+                psum.tile([P, BANK], F32, name=f"ga{h}_{c}", tag=f"ga{c}"),
+                psum.tile([P, BANK], F32, name=f"ha{h}_{c}", tag=f"ha{c}"),
+            )
 
         def wg_pass(a, h, c):
             rows = half_cols[h]
@@ -172,14 +176,12 @@ def tile_list_hwayt_dl_gelu_kernel(
             rows = half_cols[h]
             table_pass(banks[h, c][1], whd_mx[a][1][:, rows].bitcast(FP8X4), whd_mx[a][2][:, rows], a, c, False, a == 1)
 
-        tanh_half = {}
         keep_share = {}
         made = {}
 
-        def gate_tanh(h, c, tag):
-            tanh_half[h, c] = keep.tile([P, BANK], F32, name=f"tanh_half{h}_{c}", tag=tag)
+        def gate_tanh(h, c):
             nc.scalar.activation(
-                tanh_half[h, c][:], banks[h, c][0][:], ACT.Tanh, bias=half_bias[:, h : h + 1], scale=0.5
+                tanh_half[h, c], banks[h, c][0][:], ACT.Tanh, bias=half_bias[:, h : h + 1], scale=0.5
             )
 
         def gelu(h, c):
@@ -188,24 +190,32 @@ def tile_list_hwayt_dl_gelu_kernel(
 
         def gate_rest(h, c):
             keep_share[h, c] = keep.tile([P, BANK], F32, name=f"keep_share{h}_{c}", tag=f"keep_share{h}_{c}")
-            nc.scalar.activation(keep_share[h, c][:], tanh_half[h, c][:], ACT.Copy, bias=0.5, scale=-0.5)
+            size = 1.0 if h * CHUNKS + c in SUMMED_IN_PSUM else 0.5
+            nc.scalar.activation(keep_share[h, c][:], tanh_half[h, c], ACT.Copy, bias=size, scale=-size)
 
         for c in range(CHUNKS):
             open_banks(0, c)
             wh4_pass(0, 0, c)
-            whd_pass(0, 0, c)
             wg_pass(0, 0, c)
 
-        round_weight(whd_raw1[:], whd_mx[1])
+        for a in range(PASSES):
+            round_weight(whd_raw[:, a], whd_mx[a])
+        tanh_tiles = [
+            keep.tile([P, CHUNKS, BANK], F32, name="tanh_half0", tag="wg_raw"),
+            keep.tile([P, CHUNKS, BANK], F32, name="tanh_half1"),
+        ]
+        tanh_half = {(h, c): tanh_tiles[h][:, c, :] for h in range(HALVES) for c in range(CHUNKS)}
         for c in range(3):
             gather_second_words(c, f"picked_words1_{c}")
-        quantise_weight(whd_mx[1])
+        for a in range(PASSES):
+            quantise_weight(whd_mx[a])
         gather_second_words(3, "whd1_bf16")
         for c in range(2):
             wg_pass(1, 0, c)
             wh4_pass(1, 0, c)
-            gate_tanh(0, c, "whd_raw" if c == 0 else f"tanh_half0_{c}")
+            gate_tanh(0, c)
         for c in range(2):
+            whd_pass(0, 0, c)
             whd_pass(1, 0, c)
             gelu(0, c)
         for c in range(2):
@@ -217,8 +227,9 @@ def tile_list_hwayt_dl_gelu_kernel(
         for c in range(2, CHUNKS):
             wg_pass(1, 0, c)
             wh4_pass(1, 0, c)
+            whd_pass(0, 0, c)
             whd_pass(1, 0, c)
-            gate_tanh(0, c, f"tanh_half0_{c}")
+            gate_tanh(0, c)
             gelu(0, c)
             gate_rest(0, c)
         for c in range(CHUNKS):
@@ -228,7 +239,7 @@ def tile_list_hwayt_dl_gelu_kernel(
             for a in range(PASSES):
                 wh4_pass(a, 1, c)
                 whd_pass(a, 1, c)
-            gate_tanh(1, c, f"tanh_half1_{c}")
+            gate_tanh(1, c)
             gelu(1, c)
             gate_rest(1, c)
 
@@ -255,11 +266,35 @@ def tile_list_hwayt_dl_gelu_kernel(
                 old_part[u][:], listed(carried[h][:], j0, count), keep_share[bank][:, cols], ALU.mult
             )
 
-        def finish(u, tag):
+        def finish(u, result):
             h, j0, count = PIECES[u]
-            result = keep.tile([P, count], F32, name=f"result{u}", tag=tag)
-            nc.vector.scalar_tensor_tensor(result[:], new_part[u][:], 0.5, old_part[u][:], ALU.mult, ALU.add)
-            nc.sync.dma_start(out[h * P : (h + 1) * P, j0 : j0 + count], result[:])
+            nc.vector.scalar_tensor_tensor(result, new_part[u][:], 0.5, old_part[u][:], ALU.mult, ALU.add)
+            nc.sync.dma_start(out[h * P : (h + 1) * P, j0 : j0 + count], result)
+
+        flipped = {}
+
+        def sum_flipped(u, bank):
+            acc = psum.tile([P, BANK], F32, name=f"flipped_sum{u}", tag=f"ga{bank}")
+            for b in range(BANK // P):
+                cols = slice(b * P, (b + 1) * P)
+                nc.tensor.matmul(
+                    acc[:, cols], new_part[u][:, cols], identity[:], start=True, stop=False, is_transpose=True
+                )
+                nc.tensor.matmul(
+                    acc[:, cols], old_part[u][:, cols], identity[:], start=False, stop=True, is_transpose=True
+                )
+            flipped[u] = keep.tile([P, BANK], F32, name=f"flipped{u}")
+            nc.scalar.copy(flipped[u][:], acc[:])
+
+        def flip_back(u, bank):
+            h, j0, count = PIECES[u]
+            acc = psum.tile([P, BANK], F32, name=f"sum{u}", tag=f"ha{bank}")
+            for b in range(BANK // P):
+                cols = slice(b * P, (b + 1) * P)
+                nc.tensor.transpose(acc[:, cols], flipped[u][:, cols], identity[:])
+            result = keep.tile([P, BANK], F32, name=f"result{u}")
+            nc.scalar.activation(result[:], acc[:], ACT.Copy, scale=0.5)
+            nc.scalar.dma_start(out[h * P : (h + 1) * P, j0 : j0 + count], result[:])
 
         last = len(PIECES) - 1
         new_share(0)
@@ -267,11 +302,18 @@ def tile_list_hwayt_dl_gelu_kernel(
         old_share(0)
         for u in range(1, last - 1):
             old_share(u)
-            finish(u - 1, "tanh_half%d_%d" % bank_of(u)[0])
+            if u - 1 not in SUMMED_IN_PSUM:
+                finish(u - 1, tanh_half[bank_of(u)[0]])
             new_share(u + 1)
+            if u == SUMMED_IN_PSUM[-1]:
+                sum_flipped(SUMMED_IN_PSUM[0], 0)
+                for bank in range(1, len(SUMMED_IN_PSUM)):
+                    sum_flipped(SUMMED_IN_PSUM[bank], bank)
+                    flip_back(SUMMED_IN_PSUM[bank - 1], bank - 1)
+                flip_back(SUMMED_IN_PSUM[-1], len(SUMMED_IN_PSUM) - 1)
         new_share(last)
         old_share(last - 1)
-        finish(last - 2, "tanh_half%d_%d" % bank_of(last)[0])
+        finish(last - 2, tanh_half[bank_of(last)[0]])
         old_share(last)
-        finish(last - 1, "result_last0")
-        finish(last, "result_last1")
+        finish(last - 1, tanh_half[0, 0][:, bank_of(last - 1)[1]])
+        finish(last, tanh_half[0, 0][:, bank_of(last)[1]])

from contextlib import ExitStack

import concourse.mybir as mybir
from concourse.masks import make_identity

K, N, T, J = 1024, 256, 4096, 2048
FLOPS = 3 * 2 * K * N * J

F32 = mybir.dt.float32
BF16 = mybir.dt.bfloat16
I32 = mybir.dt.int32
U32 = mybir.dt.uint32
U16 = mybir.dt.uint16
U8 = mybir.dt.uint8
FP8X4 = mybir.dt.float8_e4m3fn_x4
FP4X4 = mybir.dt.float4_e2m1fn_x4
ACT = mybir.ActivationFunctionType
ALU = mybir.AluOpType

P = 128
PACK = 4
PASSES = K // (P * PACK)
HALVES = N // P
BANK = 512
CHUNKS = J // BANK
LIST_ROWS = 16
SCALE_ROWS = 16
SCALE_BASE = P - PASSES * SCALE_ROWS
SUMMED_IN_PSUM = (2, 3, 4)
PIECES = [(0, 0, 512), (0, 512, 512), (0, 1024, 512), (0, 1536, 512), (1, 0, 512), (1, 512, 512), (1, 1024, 512), (1, 1536, 256), (1, 1792, 256)]


def tile_list_hwayt_dl_gelu_kernel(
    tc, tab_words, tab_scales, wg, wh4_words, wh4_scales, whd, bg, rT, offs, out
):
    nc = tc.nc
    with ExitStack() as ctx:
        keep = ctx.enter_context(tc.tile_pool(name="keep", bufs=1))
        psum = ctx.enter_context(tc.psum_pool(name="psum", bufs=1))

        offsets = keep.tile([P, J // LIST_ROWS], U16, name="offsets")

        def listed(window, j0, count):
            return window.indirect(offsets[:, j0 // LIST_ROWS : (j0 + count) // LIST_ROWS])

        nc.sync.dma_start(offsets[:], offs)
        scale_window = keep.tile([P, T // 4], I32, name="scale_window", tag="window1", align_bytes=64)
        nc.sync.dma_start(scale_window[SCALE_BASE:P, :], tab_scales.rearrange("a q t -> (a q) t").bitcast(I32))
        wh4_planes = keep.tile([P, PASSES, N], U8, name="wh4_planes", align_bytes=64)
        nc.vector.memset(wh4_planes[:].bitcast(I32), 0)
        nc.vector.memset(scale_window[0:SCALE_BASE, :], 0)

        warm = keep.tile([P, 8], F32, name="warm")
        nc.gpsimd.memset(warm[:], 0.0)
        nc.scalar.activation(warm[:, 4:5], warm[:, 0:1], ACT.Gelu_apprx_tanh)

        identity = keep.tile([P, P], F32, name="identity")
        make_identity(nc, identity[:])

        def load_words(a):
            window = keep.tile([P, T], I32, name=f"word_window{a}", tag=f"window{a}", align_bytes=64)
            nc.sync.dma_start(window[:], tab_words[a].rearrange("p t i -> p (t i)").bitcast(I32))
            return window

        def mx_tiles(name):
            grouped = keep.tile([P, N, PACK], BF16, name=f"{name}_bf16", tag=f"{name}_bf16", align_bytes=64)
            codes = keep.tile([P, N], U32, name=f"{name}_codes", align_bytes=64)
            scales = keep.tile([P, N], U8, name=f"{name}_scales", align_bytes=64)
            return grouped, codes, scales

        def round_weight(raw, mx):
            nc.scalar.copy(
                mx[0][:].rearrange("p (c e) i -> p c i e", e=4),
                raw.rearrange("p i (c e) -> p c i e", e=4),
            )

        def quantise_weight(mx):
            nc.vector.quantize_mx(
                out=mx[1][:].bitcast(FP8X4), scales=mx[2][:], in_=mx[0][:].rearrange("p n i -> p (n i)")
            )

        word_window0 = load_words(0)

        wh4_codes = keep.tile([P, PASSES, 2 * N], U8, name="wh4_codes", align_bytes=64)
        bias = keep.tile([P, HALVES], F32, name="bias")
        half_bias = keep.tile([P, HALVES], F32, name="half_bias")
        nc.sync.dma_start(wh4_codes[:].bitcast(I32), wh4_words.rearrange("a p n -> p a n").bitcast(I32))
        wh4_rows = wh4_scales.bitcast(I32).rearrange("a (q r) n -> r q a n", r=4)
        for r in range(4):
            nc.sync.dma_start(wh4_planes[r:P:32, :, :].bitcast(I32), wh4_rows[r])
        wg_raw = keep.tile([P, PASSES, PACK, N], F32, name="wg_raw", tag="wg_raw")
        nc.sync.dma_start(wg_raw[:], wg.rearrange("(a p i) n -> p a i n", p=P, i=PACK))
        with nc.allow_non_contiguous_dma(reason="one bias value a partition"):
            nc.gpsimd.dma_start(bias[:], bg.rearrange("(h p) -> p h", p=P))
        nc.gpsimd.tensor_scalar(half_bias[:], bias[:], 0.5, 0.0, ALU.mult, ALU.add)

        tab_planes = [keep.tile([P, J], U8, name=f"tab_plane{a}", align_bytes=64) for a in range(PASSES)]
        for a in range(PASSES):
            nc.vector.memset(tab_planes[a][:].bitcast(I32), 0)

        picked_scales = keep.tile([P, J], U8, name="picked_scales", align_bytes=64)
        nc.vector.tensor_copy(picked_scales[:], listed(scale_window[:].bitcast(U8), 0, J))

        def move_plane(a):
            first = SCALE_BASE + a * SCALE_ROWS
            for r in range(4):
                nc.sync.dma_start(
                    tab_planes[a][r:P:32, :].bitcast(I32),
                    picked_scales[first + r : first + SCALE_ROWS : 4, :].bitcast(I32),
                )

        move_plane(0)
        word_window1 = load_words(1)
        move_plane(1)

        picked_words = {}

        def gather_first_words():
            picked = keep.tile([P, J], U32, name="picked_words0", align_bytes=64)
            nc.vector.tensor_copy(picked[:], listed(word_window0[:].bitcast(U32), 0, J))
            for c in range(CHUNKS):
                picked_words[0, c] = picked[:, c * BANK : (c + 1) * BANK]

        def gather_second_words(c, tag):
            picked = keep.tile([P, BANK], U32, name=f"picked_words1_{c}", tag=tag, align_bytes=64)
            nc.vector.tensor_copy(picked[:], listed(word_window1[:].bitcast(U32), c * BANK, BANK))
            picked_words[1, c] = picked[:]

        wg_mx = [mx_tiles(f"wg{a}") for a in range(PASSES)]
        whd_mx = [mx_tiles(f"whd{a}") for a in range(PASSES)]
        half_cols = [slice(h * P, (h + 1) * P) for h in range(HALVES)]

        for a in range(PASSES):
            round_weight(wg_raw[:, a], wg_mx[a])
        gather_first_words()
        for a in range(PASSES):
            quantise_weight(wg_mx[a])

        whd_raw = keep.tile([P, PASSES, PACK, N], F32, name="whd_raw", tag="wg_raw")
        for a in range(PASSES):
            nc.sync.dma_start(
                whd_raw[:, a], whd[a * P * PACK : (a + 1) * P * PACK, :].rearrange("(p i) n -> p i n", i=PACK)
            )
        carried = [keep.tile([P, T], F32, name="carried0", tag="window0", align_bytes=64)]
        nc.sync.dma_start(carried[0][:], rT[0:P, :])

        def table_pass(acc, codes, scales, a, c, start, stop):
            cols = slice(c * BANK, (c + 1) * BANK)
            nc.tensor.matmul_mx(
                out=acc[:],
                lhsT=codes,
                lhsT_scale=scales,
                rhs=picked_words[a, c].bitcast(FP8X4),
                rhs_scale=tab_planes[a][:, cols],
                start=start,
                stop=stop,
            )

        banks = {}

        def open_banks(h, c):
            banks[h, c] = (
                psum.tile([P, BANK], F32, name=f"ga{h}_{c}", tag=f"ga{c}"),
                psum.tile([P, BANK], F32, name=f"ha{h}_{c}", tag=f"ha{c}"),
            )

        def wg_pass(a, h, c):
            rows = half_cols[h]
            table_pass(banks[h, c][0], wg_mx[a][1][:, rows].bitcast(FP8X4), wg_mx[a][2][:, rows], a, c, a == 0, a == 1)

        def wh4_pass(a, h, c):
            codes = wh4_codes[:, a, 2 * h * P : 2 * (h + 1) * P].bitcast(FP4X4)
            table_pass(banks[h, c][1], codes, wh4_planes[:, a, half_cols[h]], a, c, a == 0, False)

        def whd_pass(a, h, c):
            rows = half_cols[h]
            table_pass(banks[h, c][1], whd_mx[a][1][:, rows].bitcast(FP8X4), whd_mx[a][2][:, rows], a, c, False, a == 1)

        keep_share = {}
        made = {}

        def gate_tanh(h, c):
            nc.scalar.activation(
                tanh_half[h, c], banks[h, c][0][:], ACT.Tanh, bias=half_bias[:, h : h + 1], scale=0.5
            )

        def gelu(h, c):
            made[h, c] = keep.tile([P, BANK], F32, name=f"made{h}_{c}")
            nc.scalar.activation(made[h, c][:], banks[h, c][1][:], ACT.Gelu_apprx_tanh)

        def gate_rest(h, c):
            keep_share[h, c] = keep.tile([P, BANK], F32, name=f"keep_share{h}_{c}", tag=f"keep_share{h}_{c}")
            size = 1.0 if h * CHUNKS + c in SUMMED_IN_PSUM else 0.5
            nc.scalar.activation(keep_share[h, c][:], tanh_half[h, c], ACT.Copy, bias=size, scale=-size)

        for c in range(CHUNKS):
            open_banks(0, c)
            wh4_pass(0, 0, c)
            wg_pass(0, 0, c)

        for a in range(PASSES):
            round_weight(whd_raw[:, a], whd_mx[a])
        tanh_tiles = [
            keep.tile([P, CHUNKS, BANK], F32, name="tanh_half0", tag="wg_raw"),
            keep.tile([P, CHUNKS, BANK], F32, name="tanh_half1"),
        ]
        tanh_half = {(h, c): tanh_tiles[h][:, c, :] for h in range(HALVES) for c in range(CHUNKS)}
        for c in range(3):
            gather_second_words(c, f"picked_words1_{c}")
        for a in range(PASSES):
            quantise_weight(whd_mx[a])
        gather_second_words(3, "whd1_bf16")
        for c in range(2):
            wg_pass(1, 0, c)
            wh4_pass(1, 0, c)
            gate_tanh(0, c)
        for c in range(2):
            whd_pass(0, 0, c)
            whd_pass(1, 0, c)
            gelu(0, c)
        for c in range(2):
            gate_rest(0, c)

        carried.append(keep.tile([P, T], F32, name="carried1", tag="window1", align_bytes=64))
        nc.sync.dma_start(carried[1][:], rT[P : 2 * P, :])

        for c in range(2, CHUNKS):
            wg_pass(1, 0, c)
            wh4_pass(1, 0, c)
            whd_pass(0, 0, c)
            whd_pass(1, 0, c)
            gate_tanh(0, c)
            gelu(0, c)
            gate_rest(0, c)
        for c in range(CHUNKS):
            open_banks(1, c)
            for a in range(PASSES):
                wg_pass(a, 1, c)
            for a in range(PASSES):
                wh4_pass(a, 1, c)
                whd_pass(a, 1, c)
            gate_tanh(1, c)
            gelu(1, c)
            gate_rest(1, c)

        new_part = {}
        old_part = {}

        def bank_of(u):
            h, j0, count = PIECES[u]
            return (h, j0 // BANK), slice(j0 % BANK, j0 % BANK + count)

        def new_share(u):
            bank, cols = bank_of(u)
            tag = "keep_share%d_%d" % bank_of(u - 2)[0] if 2 <= u < len(PIECES) - 1 else f"new_part{u}"
            new_part[u] = keep.tile([P, PIECES[u][2]], F32, name=f"new_part{u}", tag=tag)
            nc.vector.scalar_tensor_tensor(
                new_part[u][:], tanh_half[bank][:, cols], 1.0, made[bank][:, cols], ALU.add, ALU.mult
            )

        def old_share(u):
            h, j0, count = PIECES[u]
            bank, cols = bank_of(u)
            old_part[u] = keep.tile([P, count], F32, name=f"old_part{u}")
            nc.vector.tensor_tensor(
                old_part[u][:], listed(carried[h][:], j0, count), keep_share[bank][:, cols], ALU.mult
            )

        def finish(u, result):
            h, j0, count = PIECES[u]
            nc.vector.scalar_tensor_tensor(result, new_part[u][:], 0.5, old_part[u][:], ALU.mult, ALU.add)
            nc.sync.dma_start(out[h * P : (h + 1) * P, j0 : j0 + count], result)

        flipped = {}

        def sum_flipped(u, bank):
            acc = psum.tile([P, BANK], F32, name=f"flipped_sum{u}", tag=f"ga{bank}")
            for b in range(BANK // P):
                cols = slice(b * P, (b + 1) * P)
                nc.tensor.matmul(
                    acc[:, cols], new_part[u][:, cols], identity[:], start=True, stop=False, is_transpose=True
                )
                nc.tensor.matmul(
                    acc[:, cols], old_part[u][:, cols], identity[:], start=False, stop=True, is_transpose=True
                )
            flipped[u] = keep.tile([P, BANK], F32, name=f"flipped{u}")
            nc.scalar.copy(flipped[u][:], acc[:])

        def flip_back(u, bank):
            h, j0, count = PIECES[u]
            acc = psum.tile([P, BANK], F32, name=f"sum{u}", tag=f"ha{bank}")
            for b in range(BANK // P):
                cols = slice(b * P, (b + 1) * P)
                nc.tensor.transpose(acc[:, cols], flipped[u][:, cols], identity[:])
            result = keep.tile([P, BANK], F32, name=f"result{u}")
            nc.scalar.activation(result[:], acc[:], ACT.Copy, scale=0.5)
            nc.scalar.dma_start(out[h * P : (h + 1) * P, j0 : j0 + count], result[:])

        last = len(PIECES) - 1
        new_share(0)
        new_share(1)
        old_share(0)
        for u in range(1, last - 1):
            old_share(u)
            if u - 1 not in SUMMED_IN_PSUM:
                finish(u - 1, tanh_half[bank_of(u)[0]])
            new_share(u + 1)
            if u == SUMMED_IN_PSUM[-1]:
                sum_flipped(SUMMED_IN_PSUM[0], 0)
                for bank in range(1, len(SUMMED_IN_PSUM)):
                    sum_flipped(SUMMED_IN_PSUM[bank], bank)
                    flip_back(SUMMED_IN_PSUM[bank - 1], bank - 1)
                flip_back(SUMMED_IN_PSUM[-1], len(SUMMED_IN_PSUM) - 1)
        new_share(last)
        old_share(last - 1)
        finish(last - 2, tanh_half[bank_of(last)[0]])
        old_share(last)
        finish(last - 1, tanh_half[0, 0][:, bank_of(last - 1)[1]])
        finish(last, tanh_half[0, 0][:, bank_of(last)[1]])
